import numpy as np
import ml_dtypes


def mxq(x, axis, fmt="e4m3"):
    dtype, down = {"e4m3": (ml_dtypes.float8_e4m3fn, 7), "e5m2": (ml_dtypes.float8_e5m2, 14)}[fmt]
    v = np.moveaxis(np.asarray(x, np.float32).astype(ml_dtypes.bfloat16).astype(np.float64), axis, -1)
    blocks = v.reshape(v.shape[:-1] + (-1, 32))
    amax = np.abs(blocks).max(-1, keepdims=True)
    byte = np.maximum(np.where(amax > 0, np.frexp(amax)[1] - 1 + 127, 0) - down, 1)
    scale = np.exp2(byte - 127.0)
    codes = (blocks / scale).astype(np.float32).astype(dtype).astype(np.float64)
    return np.moveaxis((codes * scale).reshape(v.shape), -1, axis)


WIDE = False


def mx_kscale(k):
    if not WIDE:
        return np.ones(k)
    levels = np.array([10, -10, 5, -5, 0])
    if k % 512:
        return np.exp2(np.random.permutation(np.resize(levels, k // 32))).repeat(32)
    a = np.empty((k // 512, 16))
    for p in range(k // 512):
        a[p, :8] = np.random.permutation(np.resize(levels, 8))
        for g in range(8):
            far = levels[np.abs(levels - a[p, g]) >= 10]
            a[p, g + 8] = far[np.random.randint(len(far))]
    return np.exp2(a.ravel()).repeat(32)


def f64(x):
    return np.asarray(x).astype(np.float64)


def striped8(idx):
    return np.asarray(idx).reshape(8, -1, 16).transpose(0, 2, 1).reshape(128, -1).astype(np.uint16)


def unstriped8(offs):
    return offs.reshape(8, 16, -1).transpose(0, 2, 1).reshape(8, -1).astype(np.int64)


def pick8(x, idx, run):
    r = np.arange(len(x))
    return x[r[:, None], idx[r % (8 * run) // run]]


E2M1 = np.array([0.0, 0.5, 1.0, 1.5, 2.0, 3.0, 4.0, 6.0, -0.0, -0.5, -1.0, -1.5, -2.0, -3.0, -4.0, -6.0])


def pack_weight(w, fmt):
    k, n = w.shape
    w = f64(np.asarray(w, np.float32).astype(ml_dtypes.bfloat16)).reshape(k // 32, 32, n)
    amax = np.abs(w).max(1)
    if fmt == "e4m3":
        byte = np.frexp(amax)[1] - 1 + 127 - 7
    else:
        mant, ex = np.frexp(amax / 6.0)
        byte = np.where(mant > 0.5, ex, ex - 1) + 127
    byte = np.clip(np.where(amax > 0, byte, 1), 1, 254)
    scaled = (w * np.exp2(127.0 - byte)[:, None, :]).reshape(k, n).astype(np.float32)
    by_word = np.ascontiguousarray(scaled.reshape(k // 512, 128, 4, n).transpose(0, 1, 3, 2))
    if fmt == "e4m3":
        words = by_word.astype(ml_dtypes.float8_e4m3fn).view(np.uint8)
    else:
        c = by_word.astype(ml_dtypes.float4_e2m1fn).view(np.uint8) & 0xF
        words = (c[..., 0::2] | (c[..., 1::2] << 4)).reshape(k // 512, 128, 2 * n)
    return np.ascontiguousarray(words), np.ascontiguousarray(byte.astype(np.uint8).reshape(k // 512, 16, n))


def unpack_weight(words, scales, fmt):
    g, _, n = scales.shape
    words = np.ascontiguousarray(words).reshape(g, 128, n, -1)
    if fmt == "e4m3":
        vals = words.view(ml_dtypes.float8_e4m3fn).astype(np.float64)
    else:
        nib = np.empty((g, 128, n, 4), np.uint8)
        nib[..., 0::2] = words & 0xF
        nib[..., 1::2] = words >> 4
        vals = E2M1[nib]
    vals = vals * np.repeat(np.exp2(scales.astype(np.float64) - 127.0), 8, axis=1)[..., None]
    return vals.transpose(0, 1, 3, 2).reshape(g * 512, n)


D, V, Q, I = 512, 2048, 128, 512


def setup_inputs():
    n = np.random.standard_normal
    idx = np.stack([np.random.permutation(V)[:I] for _ in range(8)])
    fd = mx_kscale(D)
    vocp = pack_weight(n((D, V)) / fd[:, None], "e4m3")
    return {
        "hid": (n((D, Q)) * 1.0 / np.sqrt(D) * fd[:, None]).astype(np.float32),
        "voc_words": vocp[0],
        "voc_scales": vocp[1],
        "th": (np.random.uniform(0.0003, 0.001, (Q, 1))).astype(np.float32),
        "sw": (np.random.uniform(0.5, 2.0, (1, I))).astype(np.float32),
        "old": (0.5 * n((Q, V))).astype(np.float32),
        "offs": striped8(idx),
    }


def reference(hid, voc_words, voc_scales, th, sw, old, offs):
    idx = unstriped8(offs)
    vocu = unpack_weight(voc_words, voc_scales, "e4m3")
    hidq = mxq(f64(hid), 0, "e4m3")
    a = hidq.T @ vocu
    m1 = np.max(a, axis=1, keepdims=True)
    p = np.exp(a - m1)
    z = np.sum(p, axis=1, keepdims=True)
    px = np.exp(pick8(a, idx, 16) - m1)
    dpx = f64(sw) / (px + z * f64(th)) - f64(sw) * px / np.square(px + z * f64(th))
    dz = np.sum(f64(sw) * px / np.square(px + z * f64(th)) * (-1.0), axis=1, keepdims=True) * f64(th)
    e1 = dpx * px
    s1 = np.zeros((Q, V))
    s1[np.arange(Q)[:, None], idx[np.arange(Q) % 128 // 16]] = e1
    da = dz * p + s1
    y = da * 2.0 + f64(old)
    return y

@@ -1,0 +1,237 @@
+from contextlib import ExitStack
+
+import concourse.mybir as mybir
+from concourse.masks import make_identity
+
+D, V, Q, I = 512, 2048, 128, 512
+FLOPS = 2 * D * V * Q
+
+F32 = mybir.dt.float32
+BF16 = mybir.dt.bfloat16
+I32 = mybir.dt.int32
+U32 = mybir.dt.uint32
+U16 = mybir.dt.uint16
+U8 = mybir.dt.uint8
+FP8X4 = mybir.dt.float8_e4m3fn_x4
+ALU = mybir.AluOpType
+ACT = mybir.ActivationFunctionType
+
+P = 128
+PACK = 4
+BANK = 512
+SCORE_WIDTHS = [256,256,512,512,512]
+LOAD_WIDTHS = [512,512,512,512]
+GATHER_WIDTHS = [512]
+ROUTES = ["g","G","p","p"]
+STORE_WIDTHS = [512,512,512,256,256]
+
+
+def runs(widths):
+    start = 0
+    result = []
+    for width in widths:
+        result.append((start, start + width))
+        start = start + width
+    return result
+
+
+def tile_attend_bpresence_heads_kernel(tc, hid, voc_words, voc_scales, th, sw, old, offs, out):
+    nc = tc.nc
+    pieces = runs(SCORE_WIDTHS)
+    n = len(pieces)
+    with ExitStack() as ctx:
+        keep = ctx.enter_context(tc.tile_pool(name="keep", bufs=1))
+        psum = ctx.enter_context(tc.psum_pool(name="psum", bufs=1))
+
+        def bank(k, name):
+            return psum.tile([P, BANK], F32, name=name, tag="bank%d" % k)
+
+        offsets = keep.tile([P, I // 16], U16, name="offsets")
+        voc_sc = keep.tile([P, BANK], U8, name="voc_sc", align_bytes=64)
+        nc.vector.memset(voc_sc[:].bitcast(I32), 0)
+        window = keep.tile([P, V], F32, name="window")
+        nc.vector.memset(window[:], 0.0)
+        ident = keep.tile([P, P], F32, name="ident")
+        make_identity(nc, ident[:])
+
+        hid_raw = keep.tile([P, PACK, Q], F32, name="hid_raw")
+        nc.sync.dma_start(out=hid_raw[:], in_=hid.rearrange("(p j) q -> p j q", j=PACK))
+        for quad in range(4):
+            nc.sync.dma_start(
+                out=voc_sc[32 * quad : 32 * quad + 16, :].bitcast(I32),
+                in_=voc_scales[0][4 * quad : 4 * quad + 4, :].bitcast(I32).rearrange("r (c n) -> c r n", c=4),
+            )
+        words = voc_words[0].rearrange("p n t -> p (n t)")
+        voc = []
+        for k, (lo, hi) in enumerate(runs(LOAD_WIDTHS)):
+            piece = keep.tile([P, hi - lo], U32, name="voc%d" % k, align_bytes=64)
+            nc.sync.dma_start(out=piece[:].bitcast(I32), in_=words[:, PACK * lo : PACK * hi].bitcast(I32))
+            voc.append((lo, hi, piece))
+        nc.sync.dma_start(offsets[:], offs)
+        th_col = keep.tile([P, 1], F32, name="th_col")
+        nc.sync.dma_start(out=th_col[:], in_=th)
+        sw_cols = keep.tile([P, PACK], F32, name="sw_cols")
+        nc.sync.dma_start(out=sw_cols[:], in_=sw.rearrange("o (p j) -> p (o j)", j=PACK))
+        old_sb = []
+        for k in range(V // BANK):
+            piece = keep.tile([P, BANK], F32, name="old%d" % k)
+            nc.sync.dma_start(out=piece[:], in_=old[:, k * BANK : (k + 1) * BANK])
+            old_sb.append(piece)
+
+        grouped = keep.tile([P, Q, PACK], BF16, name="grouped", align_bytes=64)
+        nc.vector.tensor_copy(out=grouped[:], in_=hid_raw[:].rearrange("p j q -> p q j"))
+        hid_codes = keep.tile([P, Q], U32, name="hid_codes", align_bytes=64)
+        hid_sc = keep.tile([P, Q], U8, name="hid_sc", align_bytes=64)
+        nc.vector.quantize_mx(out=hid_codes[:].bitcast(FP8X4), scales=hid_sc[:], in_=grouped[:].rearrange("p q j -> p (q j)"))
+
+        scores = keep.tile([P, V], F32, name="scores")
+        expo = keep.tile([P, V], F32, name="expo")
+        run_max = keep.tile([P, n], F32, name="run_max")
+        neg_max = keep.tile([P, n], F32, name="neg_max")
+        part_sum = keep.tile([P, n], F32, name="part_sum")
+        for c, (lo, hi) in enumerate(pieces):
+            acc = bank(c, "acc%d" % c)
+            start, piece = [(a, t) for a, b, t in voc if a <= lo and hi <= b][0]
+            plane = lo // BANK
+            nc.tensor.matmul_mx(
+                out=acc[:, 0 : hi - lo],
+                lhsT=hid_codes[:].bitcast(FP8X4),
+                lhsT_scale=hid_sc[:],
+                rhs=piece[:, lo - start : hi - start].bitcast(FP8X4),
+                rhs_scale=voc_sc[4 * plane :, lo - plane * BANK : hi - plane * BANK],
+                start=True,
+                stop=True,
+            )
+            nc.vector.tensor_scalar(
+                scores[:, lo:hi], acc[:, 0 : hi - lo], 1.0, run_max[:, c - 2 : c - 1] if c >= 2 else None,
+                ALU.mult, ALU.max, accum_out=run_max[:, c : c + 1],
+            )
+            if c < n - 1:
+                nc.gpsimd.tensor_scalar(neg_max[:, c : c + 1], run_max[:, c : c + 1], -1.0, 0.0, ALU.mult, ALU.add)
+            else:
+                nc.gpsimd.tensor_scalar(
+                    neg_max[:, c : c + 1], run_max[:, c : c + 1], run_max[:, c - 1 : c], -1.0, ALU.max, ALU.mult
+                )
+            nc.scalar.activation(
+                expo[:, lo:hi], scores[:, lo:hi], ACT.Exp, bias=neg_max[:, c : c + 1], accum_out=part_sum[:, c : c + 1]
+            )
+        neg_m1 = neg_max[:, n - 1 : n]
+
+        sw_bank = bank(7, "sw_bank")
+        for j in range(PACK):
+            nc.tensor.transpose(sw_bank[:, j * P : (j + 1) * P], sw_cols[:, j : j + 1].to_broadcast([P, P]), ident[:])
+        sw_rows = sw_bank[:].rearrange("m (j k) -> m k j", j=PACK)
+
+        turned = {}
+        for k in range(V // BANK):
+            if ROUTES[k] == "p":
+                turned[k] = bank(k, "turned%d" % k)
+                for j in range(PACK):
+                    nc.tensor.matmul(
+                        turned[k][:, j * P : (j + 1) * P], old_sb[k][:, j * P : (j + 1) * P], ident[:],
+                        start=(j == 0), stop=False, is_transpose=True,
+                    )
+
+        rescale = keep.tile([P, n], F32, name="rescale")
+        nc.scalar.activation(rescale[:], neg_max[:], ACT.Exp, scale=-1.0, bias=neg_m1)
+        th2 = keep.tile([P, 1], F32, name="th2")
+        nc.vector.tensor_scalar(th2[:], th_col[:], 2.0, None, ALU.mult)
+
+        picked = keep.tile([P, I], F32, name="picked")
+        px = keep.tile([P, I], F32, name="px")
+        for lo, hi in runs(GATHER_WIDTHS):
+            nc.vector.tensor_copy(picked[:], scores[:].indirect(offsets[:]))
+            nc.scalar.activation(px[:, lo:hi], picked[:, lo:hi], ACT.Exp, bias=neg_m1)
+
+        terms = keep.tile([P, n], F32, name="terms")
+        t2 = keep.tile([P, 1], F32, name="t2")
+        nc.vector.scalar_tensor_tensor(terms[:], rescale[:], th2[:], part_sum[:], ALU.mult, ALU.mult, accum_out=t2[:])
+        tt = keep.tile([P, 1], F32, name="tt")
+        nc.vector.tensor_scalar(tt[:], t2[:], t2[:], None, ALU.mult)
+        tsq = keep.tile([P, 1], F32, name="tsq")
+        half = I // 2
+        halves = [(0, half), (half, I)]
+        wide = keep.tile([P, I], F32, name="wide")
+        for lo, hi in halves:
+            nc.vector.scalar_tensor_tensor(wide[:, lo:hi], px[:, lo:hi], t2[:], px[:, lo:hi], ALU.add, ALU.mult)
+        nc.vector.tensor_scalar(tsq[:], tt[:], 0.25, None, ALU.mult)
+        top = keep.tile([P, I], F32, name="top")
+        for lo, hi in halves:
+            nc.vector.scalar_tensor_tensor(
+                top[:, lo:hi].rearrange("m (k j) -> m k j", j=PACK), px[:, lo:hi].rearrange("m (k j) -> m k j", j=PACK),
+                t2[:], sw_rows[:, lo // PACK : hi // PACK, :], ALU.mult, ALU.mult,
+            )
+        terms_z = keep.tile([P, n], F32, name="terms_z")
+        z = keep.tile([P, 1], F32, name="z")
+        nc.vector.scalar_tensor_tensor(terms_z[:], rescale[:], -1.0, part_sum[:], ALU.mult, ALU.mult, accum_out=z[:])
+        inv_z = keep.tile([P, 1], F32, name="inv_z")
+        nc.vector.reciprocal(inv_z[:], z[:])
+        share = keep.tile([P, n], F32, name="share")
+        nc.vector.tensor_scalar(share[:], rescale[:], inv_z[:], None, ALU.mult)
+
+        inv = keep.tile([P, I], F32, name="inv")
+        for lo, hi in halves:
+            nc.scalar.activation(inv[:, lo:hi], wide[:, lo:hi], ACT.Abs_reciprocal_sqrt, bias=tsq[:])
+        inv_sq = keep.tile([P, half], F32, name="inv_sq")
+        nc.scalar.activation(inv_sq[:], inv[:, half:I], ACT.Square)
+        once = keep.tile([P, half], F32, name="once")
+        e2 = keep.tile([P, I], F32, name="e2")
+        e_sum = keep.tile([P, 2], F32, name="e_sum")
+        nc.vector.tensor_tensor(once[:], top[:, 0:half], inv[:, 0:half], ALU.mult)
+        nc.vector.scalar_tensor_tensor(e2[:, 0:half], once[:], 1.0, inv[:, 0:half], ALU.mult, ALU.mult, accum_out=e_sum[:, 0:1])
+        nc.vector.scalar_tensor_tensor(e2[:, half:I], top[:, half:I], 1.0, inv_sq[:], ALU.mult, ALU.mult, accum_out=e_sum[:, 1:2])
+        nc.vector.tensor_copy(window[:].indirect(offsets[:]), e2[:])
+
+        e_all = keep.tile([P, 1], F32, name="e_all")
+        nc.scalar.activation(e_all[:], e_sum[:, 0:1], ACT.Identity, bias=e_sum[:, 1:2])
+        coef = keep.tile([P, n], F32, name="coef")
+        nc.scalar.activation(coef[:], share[:], ACT.Copy, scale=e_all[:])
+
+        scaled = keep.tile([P, V], F32, name="scaled")
+        base = {}
+        final_bank = {0: 4, 1: 5, 2: 6, 3: 7}
+
+        def in_block(k):
+            return [(c, lo, hi) for c, (lo, hi) in enumerate(pieces) if lo // BANK == k]
+
+        def scale_block(k):
+            for c, lo, hi in in_block(k):
+                if ROUTES[k] == "G":
+                    nc.gpsimd.tensor_scalar(scaled[:, lo:hi], expo[:, lo:hi], coef[:, c : c + 1], 0.0, ALU.mult, ALU.add)
+                else:
+                    nc.scalar.activation(scaled[:, lo:hi], expo[:, lo:hi], ACT.Copy, scale=coef[:, c : c + 1])
+            if ROUTES[k] == "p":
+                for j in range(PACK):
+                    nc.tensor.matmul(
+                        turned[k][:, j * P : (j + 1) * P], scaled[:, k * BANK + j * P : k * BANK + (j + 1) * P], ident[:],
+                        start=False, stop=(j == PACK - 1), is_transpose=True,
+                    )
+            else:
+                base[k] = keep.tile([P, BANK], F32, name="base%d" % k)
+                nc.gpsimd.tensor_tensor(base[k][:], scaled[:, k * BANK : (k + 1) * BANK], old_sb[k][:], ALU.add)
+
+        def turn_back(k):
+            staged = keep.tile([P, BANK], F32, name="staged%d" % k)
+            nc.scalar.copy(staged[:], turned[k][:])
+            base[k] = bank(final_bank[k], "final%d" % k)
+            for j in range(PACK):
+                nc.tensor.transpose(base[k][:, j * P : (j + 1) * P], staged[:, j * P : (j + 1) * P], ident[:])
+
+        for step, k in [["s",1],["s",2],["s",3],["s",0],["t",2],["t",3]]:
+            if step == "s":
+                scale_block(k)
+            else:
+                turn_back(k)
+
+        result = keep.tile([P, V], F32, name="result")
+        for lo, hi in [[512,1024],[0,512],[1024,1536],[1536,1792],[1792,2048]]:
+            k = lo // BANK
+            if ROUTES[k] == "v" and k not in base:
+                base[k] = keep.tile([P, BANK], F32, name="base%d" % k)
+                for c, a, b in in_block(k):
+                    nc.vector.scalar_tensor_tensor(
+                        base[k][:, a - k * BANK : b - k * BANK], expo[:, a:b], coef[:, c : c + 1],
+                        old_sb[k][:, a - k * BANK : b - k * BANK], ALU.mult, ALU.add,
+                    )
+            nc.vector.tensor_tensor(result[:, lo:hi], base[k][:, lo - k * BANK : hi - k * BANK], window[:, lo:hi], ALU.add)
+            nc.sync.dma_start(out=out[:, lo:hi], in_=result[:, lo:hi])

@@ -22,7 +22,7 @@ BANK = 512
 SCORE_WIDTHS = [256,256,512,512,512]
 LOAD_WIDTHS = [512,512,512,512]
 GATHER_WIDTHS = [512]
-ROUTES = ["g","G","p","p"]
+ROUTES = ["v","p","p","p"]
 STORE_WIDTHS = [512,512,512,256,256]
 
 
@@ -109,9 +109,9 @@ def tile_attend_bpresence_heads_kernel(tc, hid, voc_words, voc_scales, th, sw, o
             if c < n - 1:
                 nc.gpsimd.tensor_scalar(neg_max[:, c : c + 1], run_max[:, c : c + 1], -1.0, 0.0, ALU.mult, ALU.add)
             else:
-                nc.gpsimd.tensor_scalar(
-                    neg_max[:, c : c + 1], run_max[:, c : c + 1], run_max[:, c - 1 : c], -1.0, ALU.max, ALU.mult
-                )
+                excess = keep.tile([P, 1], F32, name="excess")
+                nc.scalar.activation(excess[:], run_max[:, c : c + 1], ACT.Relu, bias=neg_max[:, c - 1 : c])
+                nc.scalar.activation(neg_max[:, c : c + 1], excess[:], ACT.Identity, scale=-1.0, bias=neg_max[:, c - 1 : c])
             nc.scalar.activation(
                 expo[:, lo:hi], scores[:, lo:hi], ACT.Exp, bias=neg_max[:, c : c + 1], accum_out=part_sum[:, c : c + 1]
             )
@@ -135,7 +135,7 @@ def tile_attend_bpresence_heads_kernel(tc, hid, voc_words, voc_scales, th, sw, o
         rescale = keep.tile([P, n], F32, name="rescale")
         nc.scalar.activation(rescale[:], neg_max[:], ACT.Exp, scale=-1.0, bias=neg_m1)
         th2 = keep.tile([P, 1], F32, name="th2")
-        nc.vector.tensor_scalar(th2[:], th_col[:], 2.0, None, ALU.mult)
+        nc.gpsimd.tensor_scalar(th2[:], th_col[:], 2.0, 0.0, ALU.mult, ALU.add)
 
         picked = keep.tile([P, I], F32, name="picked")
         px = keep.tile([P, I], F32, name="px")
@@ -146,28 +146,27 @@ def tile_attend_bpresence_heads_kernel(tc, hid, voc_words, voc_scales, th, sw, o
         terms = keep.tile([P, n], F32, name="terms")
         t2 = keep.tile([P, 1], F32, name="t2")
         nc.vector.scalar_tensor_tensor(terms[:], rescale[:], th2[:], part_sum[:], ALU.mult, ALU.mult, accum_out=t2[:])
-        tt = keep.tile([P, 1], F32, name="tt")
-        nc.vector.tensor_scalar(tt[:], t2[:], t2[:], None, ALU.mult)
+        terms_z = keep.tile([P, n], F32, name="terms_z")
+        z = keep.tile([P, 1], F32, name="z")
+        nc.vector.scalar_tensor_tensor(terms_z[:], rescale[:], -1.0, part_sum[:], ALU.mult, ALU.mult, accum_out=z[:])
         tsq = keep.tile([P, 1], F32, name="tsq")
+        nc.vector.tensor_scalar(tsq[:], t2[:], t2[:], 0.25, ALU.mult, ALU.mult)
         half = I // 2
         halves = [(0, half), (half, I)]
         wide = keep.tile([P, I], F32, name="wide")
+        inv_z = keep.tile([P, 1], F32, name="inv_z")
+        share = keep.tile([P, n], F32, name="share")
         for lo, hi in halves:
             nc.vector.scalar_tensor_tensor(wide[:, lo:hi], px[:, lo:hi], t2[:], px[:, lo:hi], ALU.add, ALU.mult)
-        nc.vector.tensor_scalar(tsq[:], tt[:], 0.25, None, ALU.mult)
+            if lo == 0:
+                nc.vector.reciprocal(inv_z[:], z[:])
+        nc.gpsimd.tensor_scalar(share[:], rescale[:], inv_z[:], 0.0, ALU.mult, ALU.add)
         top = keep.tile([P, I], F32, name="top")
         for lo, hi in halves:
             nc.vector.scalar_tensor_tensor(
                 top[:, lo:hi].rearrange("m (k j) -> m k j", j=PACK), px[:, lo:hi].rearrange("m (k j) -> m k j", j=PACK),
                 t2[:], sw_rows[:, lo // PACK : hi // PACK, :], ALU.mult, ALU.mult,
             )
-        terms_z = keep.tile([P, n], F32, name="terms_z")
-        z = keep.tile([P, 1], F32, name="z")
-        nc.vector.scalar_tensor_tensor(terms_z[:], rescale[:], -1.0, part_sum[:], ALU.mult, ALU.mult, accum_out=z[:])
-        inv_z = keep.tile([P, 1], F32, name="inv_z")
-        nc.vector.reciprocal(inv_z[:], z[:])
-        share = keep.tile([P, n], F32, name="share")
-        nc.vector.tensor_scalar(share[:], rescale[:], inv_z[:], None, ALU.mult)
 
         inv = keep.tile([P, I], F32, name="inv")
         for lo, hi in halves:
@@ -189,7 +188,7 @@ def tile_attend_bpresence_heads_kernel(tc, hid, voc_words, voc_scales, th, sw, o
 
         scaled = keep.tile([P, V], F32, name="scaled")
         base = {}
-        final_bank = {0: 4, 1: 5, 2: 6, 3: 7}
+        final_bank = {0: 7, 1: 4, 2: 5, 3: 6}
 
         def in_block(k):
             return [(c, lo, hi) for c, (lo, hi) in enumerate(pieces) if lo // BANK == k]
@@ -217,14 +216,14 @@ def tile_attend_bpresence_heads_kernel(tc, hid, voc_words, voc_scales, th, sw, o
             for j in range(PACK):
                 nc.tensor.transpose(base[k][:, j * P : (j + 1) * P], staged[:, j * P : (j + 1) * P], ident[:])
 
-        for step, k in [["s",1],["s",2],["s",3],["s",0],["t",2],["t",3]]:
+        for step, k in [["s",1],["s",2],["t",1],["s",3],["t",2],["t",3]]:
             if step == "s":
                 scale_block(k)
             else:
                 turn_back(k)
 
         result = keep.tile([P, V], F32, name="result")
-        for lo, hi in [[512,1024],[0,512],[1024,1536],[1536,1792],[1792,2048]]:
+        for lo, hi in [[0,512],[512,1024],[1024,1536],[1536,1792],[1792,2048]]:
             k = lo // BANK
             if ROUTES[k] == "v" and k not in base:
                 base[k] = keep.tile([P, BANK], F32, name="base%d" % k)

from contextlib import ExitStack

import concourse.mybir as mybir
from concourse.masks import make_identity

D, V, Q, I = 512, 2048, 128, 512
FLOPS = 2 * D * V * Q

F32 = mybir.dt.float32
BF16 = mybir.dt.bfloat16
I32 = mybir.dt.int32
U32 = mybir.dt.uint32
U16 = mybir.dt.uint16
U8 = mybir.dt.uint8
FP8X4 = mybir.dt.float8_e4m3fn_x4
ALU = mybir.AluOpType
ACT = mybir.ActivationFunctionType

P = 128
PACK = 4
BANK = 512
SCORE_WIDTHS = [256,256,512,512,512]
LOAD_WIDTHS = [512,512,512,512]
GATHER_WIDTHS = [512]
ROUTES = ["v","p","p","p"]
STORE_WIDTHS = [512,512,512,256,256]


def runs(widths):
    start = 0
    result = []
    for width in widths:
        result.append((start, start + width))
        start = start + width
    return result


def tile_attend_bpresence_heads_kernel(tc, hid, voc_words, voc_scales, th, sw, old, offs, out):
    nc = tc.nc
    pieces = runs(SCORE_WIDTHS)
    n = len(pieces)
    with ExitStack() as ctx:
        keep = ctx.enter_context(tc.tile_pool(name="keep", bufs=1))
        psum = ctx.enter_context(tc.psum_pool(name="psum", bufs=1))

        def bank(k, name):
            return psum.tile([P, BANK], F32, name=name, tag="bank%d" % k)

        offsets = keep.tile([P, I // 16], U16, name="offsets")
        voc_sc = keep.tile([P, BANK], U8, name="voc_sc", align_bytes=64)
        nc.vector.memset(voc_sc[:].bitcast(I32), 0)
        window = keep.tile([P, V], F32, name="window")
        nc.vector.memset(window[:], 0.0)
        ident = keep.tile([P, P], F32, name="ident")
        make_identity(nc, ident[:])

        hid_raw = keep.tile([P, PACK, Q], F32, name="hid_raw")
        nc.sync.dma_start(out=hid_raw[:], in_=hid.rearrange("(p j) q -> p j q", j=PACK))
        for quad in range(4):
            nc.sync.dma_start(
                out=voc_sc[32 * quad : 32 * quad + 16, :].bitcast(I32),
                in_=voc_scales[0][4 * quad : 4 * quad + 4, :].bitcast(I32).rearrange("r (c n) -> c r n", c=4),
            )
        words = voc_words[0].rearrange("p n t -> p (n t)")
        voc = []
        for k, (lo, hi) in enumerate(runs(LOAD_WIDTHS)):
            piece = keep.tile([P, hi - lo], U32, name="voc%d" % k, align_bytes=64)
            nc.sync.dma_start(out=piece[:].bitcast(I32), in_=words[:, PACK * lo : PACK * hi].bitcast(I32))
            voc.append((lo, hi, piece))
        nc.sync.dma_start(offsets[:], offs)
        th_col = keep.tile([P, 1], F32, name="th_col")
        nc.sync.dma_start(out=th_col[:], in_=th)
        sw_cols = keep.tile([P, PACK], F32, name="sw_cols")
        nc.sync.dma_start(out=sw_cols[:], in_=sw.rearrange("o (p j) -> p (o j)", j=PACK))
        old_sb = []
        for k in range(V // BANK):
            piece = keep.tile([P, BANK], F32, name="old%d" % k)
            nc.sync.dma_start(out=piece[:], in_=old[:, k * BANK : (k + 1) * BANK])
            old_sb.append(piece)

        grouped = keep.tile([P, Q, PACK], BF16, name="grouped", align_bytes=64)
        nc.vector.tensor_copy(out=grouped[:], in_=hid_raw[:].rearrange("p j q -> p q j"))
        hid_codes = keep.tile([P, Q], U32, name="hid_codes", align_bytes=64)
        hid_sc = keep.tile([P, Q], U8, name="hid_sc", align_bytes=64)
        nc.vector.quantize_mx(out=hid_codes[:].bitcast(FP8X4), scales=hid_sc[:], in_=grouped[:].rearrange("p q j -> p (q j)"))

        scores = keep.tile([P, V], F32, name="scores")
        expo = keep.tile([P, V], F32, name="expo")
        run_max = keep.tile([P, n], F32, name="run_max")
        neg_max = keep.tile([P, n], F32, name="neg_max")
        part_sum = keep.tile([P, n], F32, name="part_sum")
        for c, (lo, hi) in enumerate(pieces):
            acc = bank(c, "acc%d" % c)
            start, piece = [(a, t) for a, b, t in voc if a <= lo and hi <= b][0]
            plane = lo // BANK
            nc.tensor.matmul_mx(
                out=acc[:, 0 : hi - lo],
                lhsT=hid_codes[:].bitcast(FP8X4),
                lhsT_scale=hid_sc[:],
                rhs=piece[:, lo - start : hi - start].bitcast(FP8X4),
                rhs_scale=voc_sc[4 * plane :, lo - plane * BANK : hi - plane * BANK],
                start=True,
                stop=True,
            )
            nc.vector.tensor_scalar(
                scores[:, lo:hi], acc[:, 0 : hi - lo], 1.0, run_max[:, c - 2 : c - 1] if c >= 2 else None,
                ALU.mult, ALU.max, accum_out=run_max[:, c : c + 1],
            )
            if c < n - 1:
                nc.gpsimd.tensor_scalar(neg_max[:, c : c + 1], run_max[:, c : c + 1], -1.0, 0.0, ALU.mult, ALU.add)
            else:
                excess = keep.tile([P, 1], F32, name="excess")
                nc.scalar.activation(excess[:], run_max[:, c : c + 1], ACT.Relu, bias=neg_max[:, c - 1 : c])
                nc.scalar.activation(neg_max[:, c : c + 1], excess[:], ACT.Identity, scale=-1.0, bias=neg_max[:, c - 1 : c])
            nc.scalar.activation(
                expo[:, lo:hi], scores[:, lo:hi], ACT.Exp, bias=neg_max[:, c : c + 1], accum_out=part_sum[:, c : c + 1]
            )
        neg_m1 = neg_max[:, n - 1 : n]

        sw_bank = bank(7, "sw_bank")
        for j in range(PACK):
            nc.tensor.transpose(sw_bank[:, j * P : (j + 1) * P], sw_cols[:, j : j + 1].to_broadcast([P, P]), ident[:])
        sw_rows = sw_bank[:].rearrange("m (j k) -> m k j", j=PACK)

        turned = {}
        for k in range(V // BANK):
            if ROUTES[k] == "p":
                turned[k] = bank(k, "turned%d" % k)
                for j in range(PACK):
                    nc.tensor.matmul(
                        turned[k][:, j * P : (j + 1) * P], old_sb[k][:, j * P : (j + 1) * P], ident[:],
                        start=(j == 0), stop=False, is_transpose=True,
                    )

        rescale = keep.tile([P, n], F32, name="rescale")
        nc.scalar.activation(rescale[:], neg_max[:], ACT.Exp, scale=-1.0, bias=neg_m1)
        th2 = keep.tile([P, 1], F32, name="th2")
        nc.gpsimd.tensor_scalar(th2[:], th_col[:], 2.0, 0.0, ALU.mult, ALU.add)

        picked = keep.tile([P, I], F32, name="picked")
        px = keep.tile([P, I], F32, name="px")
        for lo, hi in runs(GATHER_WIDTHS):
            nc.vector.tensor_copy(picked[:], scores[:].indirect(offsets[:]))
            nc.scalar.activation(px[:, lo:hi], picked[:, lo:hi], ACT.Exp, bias=neg_m1)

        terms = keep.tile([P, n], F32, name="terms")
        t2 = keep.tile([P, 1], F32, name="t2")
        nc.vector.scalar_tensor_tensor(terms[:], rescale[:], th2[:], part_sum[:], ALU.mult, ALU.mult, accum_out=t2[:])
        terms_z = keep.tile([P, n], F32, name="terms_z")
        z = keep.tile([P, 1], F32, name="z")
        nc.vector.scalar_tensor_tensor(terms_z[:], rescale[:], -1.0, part_sum[:], ALU.mult, ALU.mult, accum_out=z[:])
        tsq = keep.tile([P, 1], F32, name="tsq")
        nc.vector.tensor_scalar(tsq[:], t2[:], t2[:], 0.25, ALU.mult, ALU.mult)
        half = I // 2
        halves = [(0, half), (half, I)]
        wide = keep.tile([P, I], F32, name="wide")
        inv_z = keep.tile([P, 1], F32, name="inv_z")
        share = keep.tile([P, n], F32, name="share")
        for lo, hi in halves:
            nc.vector.scalar_tensor_tensor(wide[:, lo:hi], px[:, lo:hi], t2[:], px[:, lo:hi], ALU.add, ALU.mult)
            if lo == 0:
                nc.vector.reciprocal(inv_z[:], z[:])
        nc.gpsimd.tensor_scalar(share[:], rescale[:], inv_z[:], 0.0, ALU.mult, ALU.add)
        top = keep.tile([P, I], F32, name="top")
        for lo, hi in halves:
            nc.vector.scalar_tensor_tensor(
                top[:, lo:hi].rearrange("m (k j) -> m k j", j=PACK), px[:, lo:hi].rearrange("m (k j) -> m k j", j=PACK),
                t2[:], sw_rows[:, lo // PACK : hi // PACK, :], ALU.mult, ALU.mult,
            )

        inv = keep.tile([P, I], F32, name="inv")
        for lo, hi in halves:
            nc.scalar.activation(inv[:, lo:hi], wide[:, lo:hi], ACT.Abs_reciprocal_sqrt, bias=tsq[:])
        inv_sq = keep.tile([P, half], F32, name="inv_sq")
        nc.scalar.activation(inv_sq[:], inv[:, half:I], ACT.Square)
        once = keep.tile([P, half], F32, name="once")
        e2 = keep.tile([P, I], F32, name="e2")
        e_sum = keep.tile([P, 2], F32, name="e_sum")
        nc.vector.tensor_tensor(once[:], top[:, 0:half], inv[:, 0:half], ALU.mult)
        nc.vector.scalar_tensor_tensor(e2[:, 0:half], once[:], 1.0, inv[:, 0:half], ALU.mult, ALU.mult, accum_out=e_sum[:, 0:1])
        nc.vector.scalar_tensor_tensor(e2[:, half:I], top[:, half:I], 1.0, inv_sq[:], ALU.mult, ALU.mult, accum_out=e_sum[:, 1:2])
        nc.vector.tensor_copy(window[:].indirect(offsets[:]), e2[:])

        e_all = keep.tile([P, 1], F32, name="e_all")
        nc.scalar.activation(e_all[:], e_sum[:, 0:1], ACT.Identity, bias=e_sum[:, 1:2])
        coef = keep.tile([P, n], F32, name="coef")
        nc.scalar.activation(coef[:], share[:], ACT.Copy, scale=e_all[:])

        scaled = keep.tile([P, V], F32, name="scaled")
        base = {}
        final_bank = {0: 7, 1: 4, 2: 5, 3: 6}

        def in_block(k):
            return [(c, lo, hi) for c, (lo, hi) in enumerate(pieces) if lo // BANK == k]

        def scale_block(k):
            for c, lo, hi in in_block(k):
                if ROUTES[k] == "G":
                    nc.gpsimd.tensor_scalar(scaled[:, lo:hi], expo[:, lo:hi], coef[:, c : c + 1], 0.0, ALU.mult, ALU.add)
                else:
                    nc.scalar.activation(scaled[:, lo:hi], expo[:, lo:hi], ACT.Copy, scale=coef[:, c : c + 1])
            if ROUTES[k] == "p":
                for j in range(PACK):
                    nc.tensor.matmul(
                        turned[k][:, j * P : (j + 1) * P], scaled[:, k * BANK + j * P : k * BANK + (j + 1) * P], ident[:],
                        start=False, stop=(j == PACK - 1), is_transpose=True,
                    )
            else:
                base[k] = keep.tile([P, BANK], F32, name="base%d" % k)
                nc.gpsimd.tensor_tensor(base[k][:], scaled[:, k * BANK : (k + 1) * BANK], old_sb[k][:], ALU.add)

        def turn_back(k):
            staged = keep.tile([P, BANK], F32, name="staged%d" % k)
            nc.scalar.copy(staged[:], turned[k][:])
            base[k] = bank(final_bank[k], "final%d" % k)
            for j in range(PACK):
                nc.tensor.transpose(base[k][:, j * P : (j + 1) * P], staged[:, j * P : (j + 1) * P], ident[:])

        for step, k in [["s",1],["s",2],["t",1],["s",3],["t",2],["t",3]]:
            if step == "s":
                scale_block(k)
            else:
                turn_back(k)

        result = keep.tile([P, V], F32, name="result")
        for lo, hi in [[0,512],[512,1024],[1024,1536],[1536,1792],[1792,2048]]:
            k = lo // BANK
            if ROUTES[k] == "v" and k not in base:
                base[k] = keep.tile([P, BANK], F32, name="base%d" % k)
                for c, a, b in in_block(k):
                    nc.vector.scalar_tensor_tensor(
                        base[k][:, a - k * BANK : b - k * BANK], expo[:, a:b], coef[:, c : c + 1],
                        old_sb[k][:, a - k * BANK : b - k * BANK], ALU.mult, ALU.add,
                    )
            nc.vector.tensor_tensor(result[:, lo:hi], base[k][:, lo - k * BANK : hi - k * BANK], window[:, lo:hi], ALU.add)
            nc.sync.dma_start(out=out[:, lo:hi], in_=result[:, lo:hi])
